import numpy as np
import ml_dtypes


def mxq(x, axis, fmt="e4m3"):
    dtype, down = {"e4m3": (ml_dtypes.float8_e4m3fn, 7), "e5m2": (ml_dtypes.float8_e5m2, 14)}[fmt]
    v = np.moveaxis(np.asarray(x, np.float32).astype(ml_dtypes.bfloat16).astype(np.float64), axis, -1)
    blocks = v.reshape(v.shape[:-1] + (-1, 32))
    amax = np.abs(blocks).max(-1, keepdims=True)
    byte = np.maximum(np.where(amax > 0, np.frexp(amax)[1] - 1 + 127, 0) - down, 1)
    scale = np.exp2(byte - 127.0)
    codes = (blocks / scale).astype(np.float32).astype(dtype).astype(np.float64)
    return np.moveaxis((codes * scale).reshape(v.shape), -1, axis)


WIDE = False


def mx_kscale(k):
    if not WIDE:
        return np.ones(k)
    levels = np.array([10, -10, 5, -5, 0])
    if k % 512:
        return np.exp2(np.random.permutation(np.resize(levels, k // 32))).repeat(32)
    a = np.empty((k // 512, 16))
    for p in range(k // 512):
        a[p, :8] = np.random.permutation(np.resize(levels, 8))
        for g in range(8):
            far = levels[np.abs(levels - a[p, g]) >= 10]
            a[p, g + 8] = far[np.random.randint(len(far))]
    return np.exp2(a.ravel()).repeat(32)


def f64(x):
    return np.asarray(x).astype(np.float64)


def striped(idx):
    return np.tile(idx.reshape(-1, 16).T, (8, 1)).astype(np.uint16)


def unstriped(offs):
    return offs[:16].T.reshape(-1).astype(np.int64)


def relu2(v):
    return np.maximum(v, 0.0) ** 2


K, T, E, C, N = 1024, 1280, 8, 256, 256
TOP = 3
PAD = 64


def by_expert(wq, xq):
    return np.concatenate([wq[e].T @ xq[:, e * C:(e + 1) * C] for e in range(E)], axis=1)


def setup_inputs():
    n = np.random.standard_normal
    s = mx_kscale(K)[:, None]
    slot_token = np.empty(E * C, np.int64); pos = np.tile(E * C + np.arange(T) % PAD, (TOP, 1)); taken = np.zeros(T, np.int64)
    liked = np.random.randn(T)
    for e in np.random.permutation(E):
        free = np.flatnonzero(taken < TOP); pick = np.random.permutation(free[np.argsort(-(liked[free] + np.random.gumbel(size=free.size)))[:C]]); slot_token[e * C:(e + 1) * C] = pick
        pos[taken[pick], pick] = e * C + np.arange(C); taken[pick] += 1
    g = np.random.uniform(0.2, 0.8, (TOP, T))
    return {
        "xT": (n((K, T)) * s).astype(np.float32),
        "w": (n((E, K, N)) / np.sqrt(K) / s[None]).astype(np.float32),
        "b": (0.3 * n((N, E))).astype(np.float32),
        "gate": np.stack([np.tile(r, (N, 1)) for r in g]).astype(np.float32),
        "offs": striped(slot_token),
        "pos1": striped(pos[0]),
        "pos2": striped(pos[1]),
        "pos3": striped(pos[2]),
    }


def reference(xT, w, b, gate, offs, pos1, pos2, pos3):
    idx = unstriped(offs)
    xq = mxq(f64(xT)[:, idx], 0, "e4m3")
    y = by_expert(mxq(f64(w), 1, "e4m3"), xq)
    y = relu2(y + np.repeat(f64(b), C, axis=1))
    y = np.concatenate([y, np.zeros((N, PAD))], axis=1)
    return sum(f64(gate[r]) * y[:, unstriped(p)] for r, p in enumerate((pos1, pos2, pos3)))

@@ -1,0 +1,228 @@
+from contextlib import ExitStack
+
+import concourse.mybir as mybir
+from concourse.masks import make_identity
+
+K, T, E, C, N = 1024, 1280, 8, 256, 256
+TOP = 3
+PAD = 64
+S = E * C
+FLOPS = 2 * S * K * N
+BYTES = 4 * (K * T + E * K * N + N * E + TOP * T + N * T) + 2 * 128 * (S + TOP * T) // 16
+
+F32 = mybir.dt.float32
+BF16 = mybir.dt.bfloat16
+I32 = mybir.dt.int32
+U32 = mybir.dt.uint32
+U16 = mybir.dt.uint16
+U8 = mybir.dt.uint8
+FP8X4 = mybir.dt.float8_e4m3fn_x4
+ACT = mybir.ActivationFunctionType
+ALU = mybir.AluOpType
+
+P = 128
+PACK = 4
+K_PASS = P * PACK
+PASSES = K // K_PASS
+HALVES = N // P
+X_CHUNK = 256
+X_CHUNKS = T // X_CHUNK
+G = 512
+GROUPS = S // G
+RUN = 4
+V_W_CASTS = {(1, 0), (1, 1), (1, 2), (1, 3)}
+GATE_AFTER = [3, 6, 7]
+V_X_CASTS = {(0, 0), (0, 2), (0, 3), (0, 4)}
+CHUNKS = [[(0, 512), (512, 1024), (1024, 1280)], [(0, 512), (512, 896), (896, 1280)]]
+
+
+def tile_moe_ecr_lin_relu2_kernel(tc, xT, w, b, gate, offs, pos1, pos2, pos3, out):
+    nc = tc.nc
+    with ExitStack() as ctx:
+        keep = ctx.enter_context(tc.tile_pool(name="keep", bufs=1))
+        raw = ctx.enter_context(tc.tile_pool(name="raw", bufs=16))
+        stage = ctx.enter_context(tc.tile_pool(name="stage", bufs=8))
+        work = ctx.enter_context(tc.tile_pool(name="work", bufs=3))
+        prod_pool = ctx.enter_context(tc.tile_pool(name="prod", bufs=6))
+        psum = ctx.enter_context(tc.psum_pool(name="psum", bufs=4))
+
+        offs_t = keep.tile([P, S // 16], U16, name="offs_t")
+        pos_t = [keep.tile([P, T // 16], U16, name=f"pos_t{r}") for r in range(TOP)]
+        bias = keep.tile([P, HALVES, E], F32, name="bias")
+        gate_t = keep.tile([P, TOP, T], F32, name="gate_t")
+        x_words = [keep.tile([P, T], U32, name=f"x_words{a}", align_bytes=64) for a in range(PASSES)]
+        x_scales = keep.tile([P, T], U8, name="x_scales", align_bytes=64)
+        y = [keep.tile([P, S + PAD], F32, name=f"y{h}") for h in range(HALVES)]
+
+        ident = keep.tile([P, P], F32, name="ident")
+        make_identity(nc, ident[:])
+        nc.vector.memset(x_scales[:].bitcast(I32), 0)
+        for h in range(HALVES):
+            nc.vector.memset(y[h][:, S:], 0.0)
+
+        x_raw = {}
+        w_raw = {}
+
+        def load_x(a, c):
+            t = raw.tile([P, PACK, X_CHUNK], F32, name="raw")
+            rows = xT[a * K_PASS:(a + 1) * K_PASS, c * X_CHUNK:(c + 1) * X_CHUNK]
+            nc.sync.dma_start(out=t[:], in_=rows.rearrange("(p j) t -> p j t", j=PACK))
+            x_raw[a, c] = t
+
+        def load_w(h, e):
+            t = raw.tile([P, PASSES, PACK, P], F32, name="raw")
+            for a in range(PASSES):
+                rows = w[e, a * K_PASS:(a + 1) * K_PASS, h * P:(h + 1) * P]
+                nc.sync.dma_start(out=t[:, a, :, :], in_=rows.rearrange("(p j) n -> p j n", j=PACK))
+            w_raw[h, e] = t
+
+        def load_gate(t0, t1):
+            nc.sync.dma_start(out=gate_t[:, :, t0:t1], in_=gate[:, 0:P, t0:t1].rearrange("r p t -> p r t"))
+
+        for a in range(PASSES):
+            for c in range(X_CHUNKS):
+                load_x(a, c)
+            if a == 0:
+                nc.sync.dma_start(offs_t[:], offs)
+        nc.sync.dma_start(out=bias[:], in_=b.rearrange("(h p) e -> p h e", p=P))
+        for e in range(E):
+            load_w(0, e)
+        for r, pos in enumerate((pos1, pos2, pos3)):
+            nc.sync.dma_start(pos_t[r][:], pos)
+        for e in range(E):
+            load_w(1, e)
+            if e in GATE_AFTER:
+                load_gate(*CHUNKS[0][GATE_AFTER.index(e)])
+
+        def interleave(on_vector, dst, src):
+            if on_vector:
+                nc.vector.tensor_copy(out=dst, in_=src)
+            else:
+                nc.scalar.copy(out=dst, in_=src)
+
+        def quantise_x(a, c):
+            g = stage.tile([P, X_CHUNK * PACK], BF16, name="grouped", align_bytes=64)
+            interleave((a, c) in V_X_CASTS,
+                       g[:].rearrange("p (c i j) -> p c j i", i=RUN, j=PACK),
+                       x_raw[a, c][:].rearrange("p j (c i) -> p c j i", i=RUN))
+            cols = slice(c * X_CHUNK, (c + 1) * X_CHUNK)
+            nc.vector.quantize_mx(out=x_words[a][:, cols].bitcast(FP8X4), scales=x_scales[4 * a:P, cols], in_=g[:])
+
+        slot_words = {}
+        slot_scales = {}
+
+        def gather_words(a, i):
+            t = keep.tile([P, G], U32, name=f"slot_words{a}_{i}", align_bytes=64)
+            nc.vector.tensor_copy(out=t[:], in_=x_words[a][:].indirect(offs_t[:, i * G // 16:(i + 1) * G // 16]))
+            slot_words[a, i] = t
+
+        def gather_scales(i):
+            t = keep.tile([P, G], U8, name=f"slot_scales{i}", align_bytes=64)
+            nc.vector.tensor_copy(out=t[:], in_=x_scales[:].indirect(offs_t[:, i * G // 16:(i + 1) * G // 16]))
+            slot_scales[i] = t
+
+        w_grouped = {}
+        w_words = {}
+        w_scales = {}
+
+        def cast_w(h, e):
+            g = stage.tile([P, PASSES * P * PACK], BF16, name="grouped", align_bytes=64)
+            interleave((h, e) in V_W_CASTS,
+                       g[:].rearrange("p (a c i j) -> p a c j i", a=PASSES, i=RUN, j=PACK),
+                       w_raw[h, e][:].rearrange("p a j (c i) -> p a c j i", i=RUN))
+            w_grouped[h, e] = g
+
+        def quantise_w(h, e):
+            words = keep.tile([P, PASSES * P], U32, name=f"w_words{h}_{e}", align_bytes=64)
+            scales = keep.tile([P, PASSES * P], U8, name=f"w_scales{h}_{e}", align_bytes=64)
+            nc.vector.quantize_mx(out=words[:].bitcast(FP8X4), scales=scales[:], in_=w_grouped[h, e][:])
+            w_words[h, e] = words
+            w_scales[h, e] = scales
+
+        rectified = {}
+
+        def multiply(h, e):
+            acc = psum.tile([P, C], F32, name="acc")
+            i, first = divmod(e * C, G)
+            cols = slice(first, first + C)
+            for a in range(PASSES):
+                nc.tensor.matmul_mx(
+                    out=acc[:],
+                    lhsT=w_words[h, e][:, a * P:(a + 1) * P].bitcast(FP8X4),
+                    lhsT_scale=w_scales[h, e][:, a * P:(a + 1) * P],
+                    rhs=slot_words[a, i][:, cols].bitcast(FP8X4),
+                    rhs_scale=slot_scales[i][4 * a:P, cols],
+                    start=(a == 0),
+                    stop=(a == PASSES - 1),
+                )
+            spare = w_raw[h, 4 if h == 1 and e < 4 else E - 1][:].rearrange("p a j n -> p (a j n)")
+            r = spare[:, (e % 4) * C:(e % 4 + 1) * C]
+            nc.scalar.activation(out=r, in_=acc[:], func=ACT.Relu, bias=bias[:, h, e:e + 1])
+            rectified[h, e] = r
+
+        def square(h, e):
+            nc.scalar.activation(out=y[h][:, e * C:(e + 1) * C], in_=rectified[h, e], func=ACT.Square)
+
+        def sum_on_tensor(prods, n):
+            turned = psum.tile([P, n], F32, name="turn")
+            for j in range(n // P):
+                cols = slice(j * P, (j + 1) * P)
+                for r in range(TOP):
+                    nc.tensor.matmul(out=turned[:, cols], lhsT=prods[r][:, cols], rhs=ident[:], is_transpose=True, start=(r == 0), stop=(r == TOP - 1))
+            sums = work.tile([P, n], F32, name="sums")
+            nc.scalar.copy(out=sums[:], in_=turned[:])
+            back = psum.tile([P, n], F32, name="turn")
+            for j in range(n // P):
+                cols = slice(j * P, (j + 1) * P)
+                nc.tensor.transpose(back[:, cols], sums[:, cols], ident[:])
+            total = work.tile([P, n], F32, name="total")
+            nc.scalar.copy(out=total[:], in_=back[:])
+            return total
+
+        def sum_on_vector(prods, n):
+            part = work.tile([P, n], F32, name="sums")
+            nc.vector.tensor_tensor(out=part[:], in0=prods[0][:], in1=prods[1][:], op=ALU.add)
+            total = work.tile([P, n], F32, name="total")
+            nc.vector.tensor_tensor(out=total[:], in0=part[:], in1=prods[2][:], op=ALU.add)
+            return total
+
+        def combine(h, t0, t1):
+            n = t1 - t0
+            prods = []
+            for r in range(TOP):
+                t = prod_pool.tile([P, n], F32, name=f"prod{r}")
+                nc.vector.tensor_tensor(out=t[:], in0=y[h][:].indirect(pos_t[r][:, t0 // 16:t1 // 16]), in1=gate_t[:, r, t0:t1], op=ALU.mult)
+                prods.append(t)
+            last = h == HALVES - 1 and t1 == T
+            total = sum_on_vector(prods, n) if last else sum_on_tensor(prods, n)
+            nc.sync.dma_start(out=out[h * P:(h + 1) * P, t0:t1], in_=total[:])
+
+        for c in range(X_CHUNKS):
+            quantise_x(0, c)
+        for c in range(X_CHUNKS):
+            quantise_x(1, c)
+        for i in range(GROUPS):
+            gather_words(0, i)
+
+        for e in range(E):
+            cast_w(0, e)
+            if e * C % G == 0:
+                gather_words(1, e * C // G)
+                gather_scales(e * C // G)
+            quantise_w(0, e)
+        for e in range(E):
+            multiply(0, e)
+            if e > 0:
+                square(0, e - 1)
+        square(0, E - 1)
+        for e in range(E):
+            cast_w(1, e)
+            quantise_w(1, e)
+        for e in range(E):
+            multiply(1, e)
+            if e > 0:
+                square(1, e - 1)
+        square(1, E - 1)
+        for h in range(HALVES):
+            for t0, t1 in CHUNKS[h]:
+                combine(h, t0, t1)

@@ -25,25 +25,25 @@ PACK = 4
 K_PASS = P * PACK
 PASSES = K // K_PASS
 HALVES = N // P
-X_CHUNK = 256
-X_CHUNKS = T // X_CHUNK
+X_UNIT = 256
+X_UNITS = T // X_UNIT
+X_LOADS = [(0, 512), (512, 1024), (1024, 1280)]
 G = 512
 GROUPS = S // G
 RUN = 4
-V_W_CASTS = {(1, 0), (1, 1), (1, 2), (1, 3)}
-GATE_AFTER = [3, 6, 7]
-V_X_CASTS = {(0, 0), (0, 2), (0, 3), (0, 4)}
-CHUNKS = [[(0, 512), (512, 1024), (1024, 1280)], [(0, 512), (512, 896), (896, 1280)]]
+SCALAR_WHOLE = 5
+V_X_CASTS = {(0, 0), (0, 2), (0, 4), (1, 3)}
+CHUNKS = [[(0, 512), (512, 1024), (1024, 1280)], [(0, 512), (512, 768), (768, 1280)]]
 
 
 def tile_moe_ecr_lin_relu2_kernel(tc, xT, w, b, gate, offs, pos1, pos2, pos3, out):
     nc = tc.nc
     with ExitStack() as ctx:
         keep = ctx.enter_context(tc.tile_pool(name="keep", bufs=1))
-        raw = ctx.enter_context(tc.tile_pool(name="raw", bufs=16))
-        stage = ctx.enter_context(tc.tile_pool(name="stage", bufs=8))
+        raw = ctx.enter_context(tc.tile_pool(name="raw", bufs=10))
+        stage = ctx.enter_context(tc.tile_pool(name="stage", bufs=6))
         work = ctx.enter_context(tc.tile_pool(name="work", bufs=3))
-        prod_pool = ctx.enter_context(tc.tile_pool(name="prod", bufs=6))
+        prod_pool = ctx.enter_context(tc.tile_pool(name="prod", bufs=5))
         psum = ctx.enter_context(tc.psum_pool(name="psum", bufs=4))
 
         offs_t = keep.tile([P, S // 16], U16, name="offs_t")
@@ -63,36 +63,34 @@ def tile_moe_ecr_lin_relu2_kernel(tc, xT, w, b, gate, offs, pos1, pos2, pos3, ou
         x_raw = {}
         w_raw = {}
 
-        def load_x(a, c):
-            t = raw.tile([P, PACK, X_CHUNK], F32, name="raw")
-            rows = xT[a * K_PASS:(a + 1) * K_PASS, c * X_CHUNK:(c + 1) * X_CHUNK]
+        def load_x(a, t0, t1):
+            t = raw.tile([P, PACK, t1 - t0], F32, name="raw")
+            rows = xT[a * K_PASS:(a + 1) * K_PASS, t0:t1]
             nc.sync.dma_start(out=t[:], in_=rows.rearrange("(p j) t -> p j t", j=PACK))
-            x_raw[a, c] = t
+            for u in range(t0 // X_UNIT, t1 // X_UNIT):
+                x_raw[a, u] = t[:, :, u * X_UNIT - t0:(u + 1) * X_UNIT - t0]
 
-        def load_w(h, e):
-            t = raw.tile([P, PASSES, PACK, P], F32, name="raw")
-            for a in range(PASSES):
-                rows = w[e, a * K_PASS:(a + 1) * K_PASS, h * P:(h + 1) * P]
-                nc.sync.dma_start(out=t[:, a, :, :], in_=rows.rearrange("(p j) n -> p j n", j=PACK))
-            w_raw[h, e] = t
+        def load_w(e):
+            t = raw.tile([P, PASSES, PACK, N], F32, name="raw")
+            nc.sync.dma_start(out=t[:].rearrange("p a j n -> p a (j n)"), in_=w[e].rearrange("(a p j) n -> p a (j n)", a=PASSES, j=PACK))
+            w_raw[e] = t
 
         def load_gate(t0, t1):
             nc.sync.dma_start(out=gate_t[:, :, t0:t1], in_=gate[:, 0:P, t0:t1].rearrange("r p t -> p r t"))
 
         for a in range(PASSES):
-            for c in range(X_CHUNKS):
-                load_x(a, c)
+            for t0, t1 in X_LOADS:
+                load_x(a, t0, t1)
             if a == 0:
                 nc.sync.dma_start(offs_t[:], offs)
-        nc.sync.dma_start(out=bias[:], in_=b.rearrange("(h p) e -> p h e", p=P))
         for e in range(E):
-            load_w(0, e)
+            load_w(e)
+            if e == 0:
+                nc.sync.dma_start(out=bias[:], in_=b.rearrange("(h p) e -> p h e", p=P))
         for r, pos in enumerate((pos1, pos2, pos3)):
             nc.sync.dma_start(pos_t[r][:], pos)
-        for e in range(E):
-            load_w(1, e)
-            if e in GATE_AFTER:
-                load_gate(*CHUNKS[0][GATE_AFTER.index(e)])
+        for t0, t1 in CHUNKS[0]:
+            load_gate(t0, t1)
 
         def interleave(on_vector, dst, src):
             if on_vector:
@@ -101,11 +99,11 @@ def tile_moe_ecr_lin_relu2_kernel(tc, xT, w, b, gate, offs, pos1, pos2, pos3, ou
                 nc.scalar.copy(out=dst, in_=src)
 
         def quantise_x(a, c):
-            g = stage.tile([P, X_CHUNK * PACK], BF16, name="grouped", align_bytes=64)
+            g = stage.tile([P, X_UNIT * PACK], BF16, name="grouped", align_bytes=64)
             interleave((a, c) in V_X_CASTS,
                        g[:].rearrange("p (c i j) -> p c j i", i=RUN, j=PACK),
-                       x_raw[a, c][:].rearrange("p j (c i) -> p c j i", i=RUN))
-            cols = slice(c * X_CHUNK, (c + 1) * X_CHUNK)
+                       x_raw[a, c].rearrange("p j (c i) -> p c j i", i=RUN))
+            cols = slice(c * X_UNIT, (c + 1) * X_UNIT)
             nc.vector.quantize_mx(out=x_words[a][:, cols].bitcast(FP8X4), scales=x_scales[4 * a:P, cols], in_=g[:])
 
         slot_words = {}
@@ -121,56 +119,68 @@ def tile_moe_ecr_lin_relu2_kernel(tc, xT, w, b, gate, offs, pos1, pos2, pos3, ou
             nc.vector.tensor_copy(out=t[:], in_=x_scales[:].indirect(offs_t[:, i * G // 16:(i + 1) * G // 16]))
             slot_scales[i] = t
 
-        w_grouped = {}
         w_words = {}
         w_scales = {}
 
-        def cast_w(h, e):
-            g = stage.tile([P, PASSES * P * PACK], BF16, name="grouped", align_bytes=64)
-            interleave((h, e) in V_W_CASTS,
+        def quantise_w(e, halves):
+            first, width = halves[0] * P, len(halves) * P
+            g = stage.tile([P, PASSES * width * PACK], BF16, name="grouped", align_bytes=64)
+            interleave(e >= SCALAR_WHOLE,
                        g[:].rearrange("p (a c i j) -> p a c j i", a=PASSES, i=RUN, j=PACK),
-                       w_raw[h, e][:].rearrange("p a j (c i) -> p a c j i", i=RUN))
-            w_grouped[h, e] = g
+                       w_raw[e][:, :, :, first:first + width].rearrange("p a j (c i) -> p a c j i", i=RUN))
+            words = keep.tile([P, PASSES, width], U32, name=f"w_words{e}_{first}", align_bytes=64)
+            scales = keep.tile([P, PASSES, width], U8, name=f"w_scales{e}_{first}", align_bytes=64)
+            nc.vector.quantize_mx(out=words[:].rearrange("p a n -> p (a n)").bitcast(FP8X4), scales=scales[:].rearrange("p a n -> p (a n)"), in_=g[:])
+            for h in halves:
+                cols = slice(h * P - first, (h + 1) * P - first)
+                w_words[h, e] = words[:, :, cols]
+                w_scales[h, e] = scales[:, :, cols]
 
-        def quantise_w(h, e):
-            words = keep.tile([P, PASSES * P], U32, name=f"w_words{h}_{e}", align_bytes=64)
-            scales = keep.tile([P, PASSES * P], U8, name=f"w_scales{h}_{e}", align_bytes=64)
-            nc.vector.quantize_mx(out=words[:].bitcast(FP8X4), scales=scales[:], in_=w_grouped[h, e][:])
-            w_words[h, e] = words
-            w_scales[h, e] = scales
-
+        sums_of = {}
         rectified = {}
 
-        def multiply(h, e):
-            acc = psum.tile([P, C], F32, name="acc")
+        def multiply(h, e, acc):
             i, first = divmod(e * C, G)
             cols = slice(first, first + C)
             for a in range(PASSES):
                 nc.tensor.matmul_mx(
-                    out=acc[:],
-                    lhsT=w_words[h, e][:, a * P:(a + 1) * P].bitcast(FP8X4),
-                    lhsT_scale=w_scales[h, e][:, a * P:(a + 1) * P],
+                    out=acc,
+                    lhsT=w_words[h, e][:, a, :].bitcast(FP8X4),
+                    lhsT_scale=w_scales[h, e][:, a, :],
                     rhs=slot_words[a, i][:, cols].bitcast(FP8X4),
                     rhs_scale=slot_scales[i][4 * a:P, cols],
                     start=(a == 0),
                     stop=(a == PASSES - 1),
                 )
-            spare = w_raw[h, 4 if h == 1 and e < 4 else E - 1][:].rearrange("p a j n -> p (a j n)")
-            r = spare[:, (e % 4) * C:(e % 4 + 1) * C]
-            nc.scalar.activation(out=r, in_=acc[:], func=ACT.Relu, bias=bias[:, h, e:e + 1])
+            sums_of[h, e] = acc
+
+        def flat(t):
+            return t[:].rearrange("p a j n -> p (a j n)")
+
+        def eighths(ap):
+            return ap.rearrange("p (q c) -> p q c", q=E)
+
+        early = flat(w_raw[SCALAR_WHOLE - 1])
+        late = flat(w_raw[SCALAR_WHOLE - 2])
+
+        def rectify(h, e):
+            if (h, e) == (0, E - 1):
+                r = eighths(late)[:, :, 0:C // E]
+            else:
+                r = eighths((early, late)[h][:, e * C:(e + 1) * C])
+            nc.scalar.activation(out=r, in_=eighths(sums_of[h, e]), func=ACT.Relu, bias=bias[:, h, e:e + 1])
             rectified[h, e] = r
 
         def square(h, e):
-            nc.scalar.activation(out=y[h][:, e * C:(e + 1) * C], in_=rectified[h, e], func=ACT.Square)
+            nc.scalar.activation(out=eighths(y[h][:, e * C:(e + 1) * C]), in_=rectified[h, e], func=ACT.Square)
 
-        def sum_on_tensor(prods, n):
+        def sum_on_tensor(prods, n, sums):
             turned = psum.tile([P, n], F32, name="turn")
             for j in range(n // P):
                 cols = slice(j * P, (j + 1) * P)
                 for r in range(TOP):
                     nc.tensor.matmul(out=turned[:, cols], lhsT=prods[r][:, cols], rhs=ident[:], is_transpose=True, start=(r == 0), stop=(r == TOP - 1))
-            sums = work.tile([P, n], F32, name="sums")
-            nc.scalar.copy(out=sums[:], in_=turned[:])
+            nc.scalar.copy(out=sums, in_=turned[:])
             back = psum.tile([P, n], F32, name="turn")
             for j in range(n // P):
                 cols = slice(j * P, (j + 1) * P)
@@ -193,33 +203,39 @@ def tile_moe_ecr_lin_relu2_kernel(tc, xT, w, b, gate, offs, pos1, pos2, pos3, ou
                 t = prod_pool.tile([P, n], F32, name=f"prod{r}")
                 nc.vector.tensor_tensor(out=t[:], in0=y[h][:].indirect(pos_t[r][:, t0 // 16:t1 // 16]), in1=gate_t[:, r, t0:t1], op=ALU.mult)
                 prods.append(t)
-            last = h == HALVES - 1 and t1 == T
-            total = sum_on_vector(prods, n) if last else sum_on_tensor(prods, n)
+            if h == 0:
+                total = sum_on_tensor(prods, n, late[:, (E - 2) * C:(E - 2) * C + n])
+            elif t1 < T:
+                total = sum_on_tensor(prods, n, work.tile([P, n], F32, name="sums")[:])
+            else:
+                total = sum_on_vector(prods, n)
             nc.sync.dma_start(out=out[h * P:(h + 1) * P, t0:t1], in_=total[:])
 
-        for c in range(X_CHUNKS):
+        for c in range(X_UNITS):
             quantise_x(0, c)
-        for c in range(X_CHUNKS):
+        for c in range(X_UNITS):
             quantise_x(1, c)
         for i in range(GROUPS):
             gather_words(0, i)
 
         for e in range(E):
-            cast_w(0, e)
             if e * C % G == 0:
                 gather_words(1, e * C // G)
                 gather_scales(e * C // G)
-            quantise_w(0, e)
+            for halves in [[0, 1]] if e < E - 1 else [[0], [1]]:
+                quantise_w(e, halves)
         for e in range(E):
-            multiply(0, e)
+            multiply(0, e, psum.tile([P, C], F32, name="turn")[:])
+            rectify(0, e)
             if e > 0:
                 square(0, e - 1)
         square(0, E - 1)
+        for e in range(0, E, 2):
+            acc = psum.tile([P, 2, C], F32, name="pair")
+            for d in range(2):
+                multiply(1, e + d, acc[:, d, :])
         for e in range(E):
-            cast_w(1, e)
-            quantise_w(1, e)
-        for e in range(E):
-            multiply(1, e)
+            rectify(1, e)
             if e > 0:
                 square(1, e - 1)
         square(1, E - 1)

@@ -25,14 +25,17 @@ PACK = 4
 K_PASS = P * PACK
 PASSES = K // K_PASS
 HALVES = N // P
-X_UNIT = 256
-X_UNITS = T // X_UNIT
-X_LOADS = [(0, 512), (512, 1024), (1024, 1280)]
-G = 512
+X_LOADS = [[(0, 512), (512, 1024), (1024, 1280)], [(0, 640), (640, 1280)]]
+X_UNITS = [
+    [(0, 256, True), (256, 512, False), (512, 768, True), (768, 1024, False), (1024, 1280, True)],
+    [(0, 256, False), (256, 512, False), (512, 640, False), (640, 896, False), (896, 1152, True), (1152, 1280, True)],
+]
+G = 1024
+WINDOW = 1408
 GROUPS = S // G
 RUN = 4
+BLOCK = P * PACK
 SCALAR_WHOLE = 5
-V_X_CASTS = {(0, 0), (0, 2), (0, 4), (1, 3)}
 CHUNKS = [[(0, 512), (512, 1024), (1024, 1280)], [(0, 512), (512, 768), (768, 1280)]]
 
 
@@ -40,9 +43,9 @@ def tile_moe_ecr_lin_relu2_kernel(tc, xT, w, b, gate, offs, pos1, pos2, pos3, ou
     nc = tc.nc
     with ExitStack() as ctx:
         keep = ctx.enter_context(tc.tile_pool(name="keep", bufs=1))
-        raw = ctx.enter_context(tc.tile_pool(name="raw", bufs=10))
+        raw = ctx.enter_context(tc.tile_pool(name="raw", bufs=8))
         stage = ctx.enter_context(tc.tile_pool(name="stage", bufs=6))
-        work = ctx.enter_context(tc.tile_pool(name="work", bufs=3))
+        work = ctx.enter_context(tc.tile_pool(name="work", bufs=4))
         prod_pool = ctx.enter_context(tc.tile_pool(name="prod", bufs=5))
         psum = ctx.enter_context(tc.psum_pool(name="psum", bufs=4))
 
@@ -50,13 +53,15 @@ def tile_moe_ecr_lin_relu2_kernel(tc, xT, w, b, gate, offs, pos1, pos2, pos3, ou
         pos_t = [keep.tile([P, T // 16], U16, name=f"pos_t{r}") for r in range(TOP)]
         bias = keep.tile([P, HALVES, E], F32, name="bias")
         gate_t = keep.tile([P, TOP, T], F32, name="gate_t")
-        x_words = [keep.tile([P, T], U32, name=f"x_words{a}", align_bytes=64) for a in range(PASSES)]
-        x_scales = keep.tile([P, T], U8, name="x_scales", align_bytes=64)
+        x_words = [keep.tile([P, WINDOW], U32, name=f"x_words{a}", align_bytes=64) for a in range(PASSES)]
+        x_scales = keep.tile([P, WINDOW], U8, name="x_scales", align_bytes=64)
         y = [keep.tile([P, S + PAD], F32, name=f"y{h}") for h in range(HALVES)]
 
         ident = keep.tile([P, P], F32, name="ident")
         make_identity(nc, ident[:])
         nc.vector.memset(x_scales[:].bitcast(I32), 0)
+        for a in range(PASSES):
+            nc.vector.memset(x_words[a][:, T:].bitcast(I32), 0)
         for h in range(HALVES):
             nc.vector.memset(y[h][:, S:], 0.0)
 
@@ -67,19 +72,26 @@ def tile_moe_ecr_lin_relu2_kernel(tc, xT, w, b, gate, offs, pos1, pos2, pos3, ou
             t = raw.tile([P, PACK, t1 - t0], F32, name="raw")
             rows = xT[a * K_PASS:(a + 1) * K_PASS, t0:t1]
             nc.sync.dma_start(out=t[:], in_=rows.rearrange("(p j) t -> p j t", j=PACK))
-            for u in range(t0 // X_UNIT, t1 // X_UNIT):
-                x_raw[a, u] = t[:, :, u * X_UNIT - t0:(u + 1) * X_UNIT - t0]
+            for u0, u1, on_vector in X_UNITS[a]:
+                if t0 <= u0 < t1:
+                    x_raw[a, u0] = t[:, :, u0 - t0:u1 - t0]
 
         def load_w(e):
             t = raw.tile([P, PASSES, PACK, N], F32, name="raw")
-            nc.sync.dma_start(out=t[:].rearrange("p a j n -> p a (j n)"), in_=w[e].rearrange("(a p j) n -> p a (j n)", a=PASSES, j=PACK))
+            dst = t[:].rearrange("p a j n -> p a (j n)")
+            src = w[e].rearrange("(a p j) n -> p a (j n)", a=PASSES, j=PACK)
+            if e < E - 1:
+                nc.sync.dma_start(out=dst, in_=src)
+            else:
+                for a in range(PASSES):
+                    nc.sync.dma_start(out=dst[:, a, :], in_=src[:, a, :])
             w_raw[e] = t
 
         def load_gate(t0, t1):
             nc.sync.dma_start(out=gate_t[:, :, t0:t1], in_=gate[:, 0:P, t0:t1].rearrange("r p t -> p r t"))
 
         for a in range(PASSES):
-            for t0, t1 in X_LOADS:
+            for t0, t1 in X_LOADS[a]:
                 load_x(a, t0, t1)
             if a == 0:
                 nc.sync.dma_start(offs_t[:], offs)
@@ -98,13 +110,12 @@ def tile_moe_ecr_lin_relu2_kernel(tc, xT, w, b, gate, offs, pos1, pos2, pos3, ou
             else:
                 nc.scalar.copy(out=dst, in_=src)
 
-        def quantise_x(a, c):
-            g = stage.tile([P, X_UNIT * PACK], BF16, name="grouped", align_bytes=64)
-            interleave((a, c) in V_X_CASTS,
+        def quantise_x(a, t0, t1, on_vector):
+            g = stage.tile([P, (t1 - t0) * PACK], BF16, name="grouped", align_bytes=64)
+            interleave(on_vector,
                        g[:].rearrange("p (c i j) -> p c j i", i=RUN, j=PACK),
-                       x_raw[a, c].rearrange("p j (c i) -> p c j i", i=RUN))
-            cols = slice(c * X_UNIT, (c + 1) * X_UNIT)
-            nc.vector.quantize_mx(out=x_words[a][:, cols].bitcast(FP8X4), scales=x_scales[4 * a:P, cols], in_=g[:])
+                       x_raw[a, t0].rearrange("p j (c i) -> p c j i", i=RUN))
+            nc.vector.quantize_mx(out=x_words[a][:, t0:t1].bitcast(FP8X4), scales=x_scales[4 * a:P, t0:t1], in_=g[:])
 
         slot_words = {}
         slot_scales = {}
@@ -122,19 +133,21 @@ def tile_moe_ecr_lin_relu2_kernel(tc, xT, w, b, gate, offs, pos1, pos2, pos3, ou
         w_words = {}
         w_scales = {}
 
-        def quantise_w(e, halves):
-            first, width = halves[0] * P, len(halves) * P
-            g = stage.tile([P, PASSES * width * PACK], BF16, name="grouped", align_bytes=64)
+        def cast_w(dst, e, passes, halves):
+            src = w_raw[e][:, passes[0]:passes[-1] + 1, :, halves[0] * P:(halves[-1] + 1) * P]
             interleave(e >= SCALAR_WHOLE,
-                       g[:].rearrange("p (a c i j) -> p a c j i", a=PASSES, i=RUN, j=PACK),
-                       w_raw[e][:, :, :, first:first + width].rearrange("p a j (c i) -> p a c j i", i=RUN))
-            words = keep.tile([P, PASSES, width], U32, name=f"w_words{e}_{first}", align_bytes=64)
-            scales = keep.tile([P, PASSES, width], U8, name=f"w_scales{e}_{first}", align_bytes=64)
-            nc.vector.quantize_mx(out=words[:].rearrange("p a n -> p (a n)").bitcast(FP8X4), scales=scales[:].rearrange("p a n -> p (a n)"), in_=g[:])
-            for h in halves:
-                cols = slice(h * P - first, (h + 1) * P - first)
-                w_words[h, e] = words[:, :, cols]
-                w_scales[h, e] = scales[:, :, cols]
+                       dst.rearrange("p (a c i j) -> p a c j i", a=len(passes), i=RUN, j=PACK),
+                       src.rearrange("p a j (c i) -> p a c j i", i=RUN))
+            return [(h, e, a) for a in passes for h in halves]
+
+        def quantise_w(src, blocks):
+            name = "%d_%d_%d" % blocks[0]
+            words = keep.tile([P, len(blocks) * P], U32, name="w_words" + name, align_bytes=64)
+            scales = keep.tile([P, len(blocks) * P], U8, name="w_scales" + name, align_bytes=64)
+            nc.vector.quantize_mx(out=words[:].bitcast(FP8X4), scales=scales[:], in_=src)
+            for n, block in enumerate(blocks):
+                w_words[block] = words[:, n * P:(n + 1) * P]
+                w_scales[block] = scales[:, n * P:(n + 1) * P]
 
         sums_of = {}
         rectified = {}
@@ -145,8 +158,8 @@ def tile_moe_ecr_lin_relu2_kernel(tc, xT, w, b, gate, offs, pos1, pos2, pos3, ou
             for a in range(PASSES):
                 nc.tensor.matmul_mx(
                     out=acc,
-                    lhsT=w_words[h, e][:, a, :].bitcast(FP8X4),
-                    lhsT_scale=w_scales[h, e][:, a, :],
+                    lhsT=w_words[h, e, a].bitcast(FP8X4),
+                    lhsT_scale=w_scales[h, e, a],
                     rhs=slot_words[a, i][:, cols].bitcast(FP8X4),
                     rhs_scale=slot_scales[i][4 * a:P, cols],
                     start=(a == 0),
@@ -189,32 +202,36 @@ def tile_moe_ecr_lin_relu2_kernel(tc, xT, w, b, gate, offs, pos1, pos2, pos3, ou
             nc.scalar.copy(out=total[:], in_=back[:])
             return total
 
-        def sum_on_vector(prods, n):
-            part = work.tile([P, n], F32, name="sums")
-            nc.vector.tensor_tensor(out=part[:], in0=prods[0][:], in1=prods[1][:], op=ALU.add)
-            total = work.tile([P, n], F32, name="total")
-            nc.vector.tensor_tensor(out=total[:], in0=part[:], in1=prods[2][:], op=ALU.add)
-            return total
+        def gather_gated(h, r, t0, t1):
+            t = prod_pool.tile([P, t1 - t0], F32, name=f"prod{r}")
+            nc.vector.tensor_tensor(out=t[:], in0=y[h][:].indirect(pos_t[r][:, t0 // 16:t1 // 16]), in1=gate_t[:, r, t0:t1], op=ALU.mult)
+            return t
+
+        def store(h, t0, t1, total):
+            nc.sync.dma_start(out=out[h * P:(h + 1) * P, t0:t1], in_=total[:])
 
         def combine(h, t0, t1):
             n = t1 - t0
-            prods = []
-            for r in range(TOP):
-                t = prod_pool.tile([P, n], F32, name=f"prod{r}")
-                nc.vector.tensor_tensor(out=t[:], in0=y[h][:].indirect(pos_t[r][:, t0 // 16:t1 // 16]), in1=gate_t[:, r, t0:t1], op=ALU.mult)
-                prods.append(t)
-            if h == 0:
-                total = sum_on_tensor(prods, n, late[:, (E - 2) * C:(E - 2) * C + n])
-            elif t1 < T:
-                total = sum_on_tensor(prods, n, work.tile([P, n], F32, name="sums")[:])
-            else:
-                total = sum_on_vector(prods, n)
-            nc.sync.dma_start(out=out[h * P:(h + 1) * P, t0:t1], in_=total[:])
+            prods = [gather_gated(h, r, t0, t1) for r in range(TOP)]
+            sums = late[:, (E - 2) * C:(E - 2) * C + n] if h == 0 else work.tile([P, n], F32, name="sums")[:]
+            store(h, t0, t1, sum_on_tensor(prods, n, sums))
 
-        for c in range(X_UNITS):
-            quantise_x(0, c)
-        for c in range(X_UNITS):
-            quantise_x(1, c)
+        def combine_last(h, t0, t1):
+            mid = (t0 + t1) // 2
+            first = gather_gated(h, 0, t0, t1)
+            second = gather_gated(h, 1, t0, t1)
+            third = {t0: gather_gated(h, 2, t0, mid)}
+            part = work.tile([P, t1 - t0], F32, name="sums")
+            nc.vector.tensor_tensor(out=part[:], in0=first[:], in1=second[:], op=ALU.add)
+            third[mid] = gather_gated(h, 2, mid, t1)
+            for u0, u1 in ((t0, mid), (mid, t1)):
+                total = work.tile([P, u1 - u0], F32, name="total")
+                nc.vector.tensor_tensor(out=total[:], in0=part[:, u0 - t0:u1 - t0], in1=third[u0][:], op=ALU.add)
+                store(h, u0, u1, total)
+
+        for a in range(PASSES):
+            for t0, t1, on_vector in X_UNITS[a]:
+                quantise_x(a, t0, t1, on_vector)
         for i in range(GROUPS):
             gather_words(0, i)
 
@@ -222,8 +239,16 @@ def tile_moe_ecr_lin_relu2_kernel(tc, xT, w, b, gate, offs, pos1, pos2, pos3, ou
             if e * C % G == 0:
                 gather_words(1, e * C // G)
                 gather_scales(e * C // G)
-            for halves in [[0, 1]] if e < E - 1 else [[0], [1]]:
-                quantise_w(e, halves)
+            if e < E - 1:
+                halves = [0, 1] if e < E - 2 else [0]
+                g = stage.tile([P, PASSES * len(halves) * BLOCK], BF16, name="grouped", align_bytes=64)
+                quantise_w(g[:], cast_w(g[:], e, [0, 1], halves))
+        last = stage.tile([P, 4 * BLOCK], BF16, name="grouped", align_bytes=64)
+        for a, first in enumerate((0, 3 * BLOCK // 2)):
+            g = last[:, first:first + BLOCK]
+            quantise_w(g, cast_w(g, E - 1, [a], [0]))
+        blocks = cast_w(last[:, :2 * BLOCK], E - 2, [0, 1], [1]) + cast_w(last[:, 2 * BLOCK:], E - 1, [0, 1], [1])
+        quantise_w(last[:], blocks)
         for e in range(E):
             multiply(0, e, psum.tile([P, C], F32, name="turn")[:])
             rectify(0, e)
@@ -241,4 +266,7 @@ def tile_moe_ecr_lin_relu2_kernel(tc, xT, w, b, gate, offs, pos1, pos2, pos3, ou
         square(1, E - 1)
         for h in range(HALVES):
             for t0, t1 in CHUNKS[h]:
-                combine(h, t0, t1)
+                if h == HALVES - 1 and t1 == T:
+                    combine_last(h, t0, t1)
+                else:
+                    combine(h, t0, t1)

from contextlib import ExitStack

import concourse.mybir as mybir
from concourse.masks import make_identity

K, T, E, C, N = 1024, 1280, 8, 256, 256
TOP = 3
PAD = 64
S = E * C
FLOPS = 2 * S * K * N
BYTES = 4 * (K * T + E * K * N + N * E + TOP * T + N * T) + 2 * 128 * (S + TOP * T) // 16

F32 = mybir.dt.float32
BF16 = mybir.dt.bfloat16
I32 = mybir.dt.int32
U32 = mybir.dt.uint32
U16 = mybir.dt.uint16
U8 = mybir.dt.uint8
FP8X4 = mybir.dt.float8_e4m3fn_x4
ACT = mybir.ActivationFunctionType
ALU = mybir.AluOpType

P = 128
PACK = 4
K_PASS = P * PACK
PASSES = K // K_PASS
HALVES = N // P
X_LOADS = [[(0, 512), (512, 1024), (1024, 1280)], [(0, 640), (640, 1280)]]
X_UNITS = [
    [(0, 256, True), (256, 512, False), (512, 768, True), (768, 1024, False), (1024, 1280, True)],
    [(0, 256, False), (256, 512, False), (512, 640, False), (640, 896, False), (896, 1152, True), (1152, 1280, True)],
]
G = 1024
WINDOW = 1408
GROUPS = S // G
RUN = 4
BLOCK = P * PACK
SCALAR_WHOLE = 5
CHUNKS = [[(0, 512), (512, 1024), (1024, 1280)], [(0, 512), (512, 768), (768, 1280)]]


def tile_moe_ecr_lin_relu2_kernel(tc, xT, w, b, gate, offs, pos1, pos2, pos3, out):
    nc = tc.nc
    with ExitStack() as ctx:
        keep = ctx.enter_context(tc.tile_pool(name="keep", bufs=1))
        raw = ctx.enter_context(tc.tile_pool(name="raw", bufs=8))
        stage = ctx.enter_context(tc.tile_pool(name="stage", bufs=6))
        work = ctx.enter_context(tc.tile_pool(name="work", bufs=4))
        prod_pool = ctx.enter_context(tc.tile_pool(name="prod", bufs=5))
        psum = ctx.enter_context(tc.psum_pool(name="psum", bufs=4))

        offs_t = keep.tile([P, S // 16], U16, name="offs_t")
        pos_t = [keep.tile([P, T // 16], U16, name=f"pos_t{r}") for r in range(TOP)]
        bias = keep.tile([P, HALVES, E], F32, name="bias")
        gate_t = keep.tile([P, TOP, T], F32, name="gate_t")
        x_words = [keep.tile([P, WINDOW], U32, name=f"x_words{a}", align_bytes=64) for a in range(PASSES)]
        x_scales = keep.tile([P, WINDOW], U8, name="x_scales", align_bytes=64)
        y = [keep.tile([P, S + PAD], F32, name=f"y{h}") for h in range(HALVES)]

        ident = keep.tile([P, P], F32, name="ident")
        make_identity(nc, ident[:])
        nc.vector.memset(x_scales[:].bitcast(I32), 0)
        for a in range(PASSES):
            nc.vector.memset(x_words[a][:, T:].bitcast(I32), 0)
        for h in range(HALVES):
            nc.vector.memset(y[h][:, S:], 0.0)

        x_raw = {}
        w_raw = {}

        def load_x(a, t0, t1):
            t = raw.tile([P, PACK, t1 - t0], F32, name="raw")
            rows = xT[a * K_PASS:(a + 1) * K_PASS, t0:t1]
            nc.sync.dma_start(out=t[:], in_=rows.rearrange("(p j) t -> p j t", j=PACK))
            for u0, u1, on_vector in X_UNITS[a]:
                if t0 <= u0 < t1:
                    x_raw[a, u0] = t[:, :, u0 - t0:u1 - t0]

        def load_w(e):
            t = raw.tile([P, PASSES, PACK, N], F32, name="raw")
            dst = t[:].rearrange("p a j n -> p a (j n)")
            src = w[e].rearrange("(a p j) n -> p a (j n)", a=PASSES, j=PACK)
            if e < E - 1:
                nc.sync.dma_start(out=dst, in_=src)
            else:
                for a in range(PASSES):
                    nc.sync.dma_start(out=dst[:, a, :], in_=src[:, a, :])
            w_raw[e] = t

        def load_gate(t0, t1):
            nc.sync.dma_start(out=gate_t[:, :, t0:t1], in_=gate[:, 0:P, t0:t1].rearrange("r p t -> p r t"))

        for a in range(PASSES):
            for t0, t1 in X_LOADS[a]:
                load_x(a, t0, t1)
            if a == 0:
                nc.sync.dma_start(offs_t[:], offs)
        for e in range(E):
            load_w(e)
            if e == 0:
                nc.sync.dma_start(out=bias[:], in_=b.rearrange("(h p) e -> p h e", p=P))
        for r, pos in enumerate((pos1, pos2, pos3)):
            nc.sync.dma_start(pos_t[r][:], pos)
        for t0, t1 in CHUNKS[0]:
            load_gate(t0, t1)

        def interleave(on_vector, dst, src):
            if on_vector:
                nc.vector.tensor_copy(out=dst, in_=src)
            else:
                nc.scalar.copy(out=dst, in_=src)

        def quantise_x(a, t0, t1, on_vector):
            g = stage.tile([P, (t1 - t0) * PACK], BF16, name="grouped", align_bytes=64)
            interleave(on_vector,
                       g[:].rearrange("p (c i j) -> p c j i", i=RUN, j=PACK),
                       x_raw[a, t0].rearrange("p j (c i) -> p c j i", i=RUN))
            nc.vector.quantize_mx(out=x_words[a][:, t0:t1].bitcast(FP8X4), scales=x_scales[4 * a:P, t0:t1], in_=g[:])

        slot_words = {}
        slot_scales = {}

        def gather_words(a, i):
            t = keep.tile([P, G], U32, name=f"slot_words{a}_{i}", align_bytes=64)
            nc.vector.tensor_copy(out=t[:], in_=x_words[a][:].indirect(offs_t[:, i * G // 16:(i + 1) * G // 16]))
            slot_words[a, i] = t

        def gather_scales(i):
            t = keep.tile([P, G], U8, name=f"slot_scales{i}", align_bytes=64)
            nc.vector.tensor_copy(out=t[:], in_=x_scales[:].indirect(offs_t[:, i * G // 16:(i + 1) * G // 16]))
            slot_scales[i] = t

        w_words = {}
        w_scales = {}

        def cast_w(dst, e, passes, halves):
            src = w_raw[e][:, passes[0]:passes[-1] + 1, :, halves[0] * P:(halves[-1] + 1) * P]
            interleave(e >= SCALAR_WHOLE,
                       dst.rearrange("p (a c i j) -> p a c j i", a=len(passes), i=RUN, j=PACK),
                       src.rearrange("p a j (c i) -> p a c j i", i=RUN))
            return [(h, e, a) for a in passes for h in halves]

        def quantise_w(src, blocks):
            name = "%d_%d_%d" % blocks[0]
            words = keep.tile([P, len(blocks) * P], U32, name="w_words" + name, align_bytes=64)
            scales = keep.tile([P, len(blocks) * P], U8, name="w_scales" + name, align_bytes=64)
            nc.vector.quantize_mx(out=words[:].bitcast(FP8X4), scales=scales[:], in_=src)
            for n, block in enumerate(blocks):
                w_words[block] = words[:, n * P:(n + 1) * P]
                w_scales[block] = scales[:, n * P:(n + 1) * P]

        sums_of = {}
        rectified = {}

        def multiply(h, e, acc):
            i, first = divmod(e * C, G)
            cols = slice(first, first + C)
            for a in range(PASSES):
                nc.tensor.matmul_mx(
                    out=acc,
                    lhsT=w_words[h, e, a].bitcast(FP8X4),
                    lhsT_scale=w_scales[h, e, a],
                    rhs=slot_words[a, i][:, cols].bitcast(FP8X4),
                    rhs_scale=slot_scales[i][4 * a:P, cols],
                    start=(a == 0),
                    stop=(a == PASSES - 1),
                )
            sums_of[h, e] = acc

        def flat(t):
            return t[:].rearrange("p a j n -> p (a j n)")

        def eighths(ap):
            return ap.rearrange("p (q c) -> p q c", q=E)

        early = flat(w_raw[SCALAR_WHOLE - 1])
        late = flat(w_raw[SCALAR_WHOLE - 2])

        def rectify(h, e):
            if (h, e) == (0, E - 1):
                r = eighths(late)[:, :, 0:C // E]
            else:
                r = eighths((early, late)[h][:, e * C:(e + 1) * C])
            nc.scalar.activation(out=r, in_=eighths(sums_of[h, e]), func=ACT.Relu, bias=bias[:, h, e:e + 1])
            rectified[h, e] = r

        def square(h, e):
            nc.scalar.activation(out=eighths(y[h][:, e * C:(e + 1) * C]), in_=rectified[h, e], func=ACT.Square)

        def sum_on_tensor(prods, n, sums):
            turned = psum.tile([P, n], F32, name="turn")
            for j in range(n // P):
                cols = slice(j * P, (j + 1) * P)
                for r in range(TOP):
                    nc.tensor.matmul(out=turned[:, cols], lhsT=prods[r][:, cols], rhs=ident[:], is_transpose=True, start=(r == 0), stop=(r == TOP - 1))
            nc.scalar.copy(out=sums, in_=turned[:])
            back = psum.tile([P, n], F32, name="turn")
            for j in range(n // P):
                cols = slice(j * P, (j + 1) * P)
                nc.tensor.transpose(back[:, cols], sums[:, cols], ident[:])
            total = work.tile([P, n], F32, name="total")
            nc.scalar.copy(out=total[:], in_=back[:])
            return total

        def gather_gated(h, r, t0, t1):
            t = prod_pool.tile([P, t1 - t0], F32, name=f"prod{r}")
            nc.vector.tensor_tensor(out=t[:], in0=y[h][:].indirect(pos_t[r][:, t0 // 16:t1 // 16]), in1=gate_t[:, r, t0:t1], op=ALU.mult)
            return t

        def store(h, t0, t1, total):
            nc.sync.dma_start(out=out[h * P:(h + 1) * P, t0:t1], in_=total[:])

        def combine(h, t0, t1):
            n = t1 - t0
            prods = [gather_gated(h, r, t0, t1) for r in range(TOP)]
            sums = late[:, (E - 2) * C:(E - 2) * C + n] if h == 0 else work.tile([P, n], F32, name="sums")[:]
            store(h, t0, t1, sum_on_tensor(prods, n, sums))

        def combine_last(h, t0, t1):
            mid = (t0 + t1) // 2
            first = gather_gated(h, 0, t0, t1)
            second = gather_gated(h, 1, t0, t1)
            third = {t0: gather_gated(h, 2, t0, mid)}
            part = work.tile([P, t1 - t0], F32, name="sums")
            nc.vector.tensor_tensor(out=part[:], in0=first[:], in1=second[:], op=ALU.add)
            third[mid] = gather_gated(h, 2, mid, t1)
            for u0, u1 in ((t0, mid), (mid, t1)):
                total = work.tile([P, u1 - u0], F32, name="total")
                nc.vector.tensor_tensor(out=total[:], in0=part[:, u0 - t0:u1 - t0], in1=third[u0][:], op=ALU.add)
                store(h, u0, u1, total)

        for a in range(PASSES):
            for t0, t1, on_vector in X_UNITS[a]:
                quantise_x(a, t0, t1, on_vector)
        for i in range(GROUPS):
            gather_words(0, i)

        for e in range(E):
            if e * C % G == 0:
                gather_words(1, e * C // G)
                gather_scales(e * C // G)
            if e < E - 1:
                halves = [0, 1] if e < E - 2 else [0]
                g = stage.tile([P, PASSES * len(halves) * BLOCK], BF16, name="grouped", align_bytes=64)
                quantise_w(g[:], cast_w(g[:], e, [0, 1], halves))
        last = stage.tile([P, 4 * BLOCK], BF16, name="grouped", align_bytes=64)
        for a, first in enumerate((0, 3 * BLOCK // 2)):
            g = last[:, first:first + BLOCK]
            quantise_w(g, cast_w(g, E - 1, [a], [0]))
        blocks = cast_w(last[:, :2 * BLOCK], E - 2, [0, 1], [1]) + cast_w(last[:, 2 * BLOCK:], E - 1, [0, 1], [1])
        quantise_w(last[:], blocks)
        for e in range(E):
            multiply(0, e, psum.tile([P, C], F32, name="turn")[:])
            rectify(0, e)
            if e > 0:
                square(0, e - 1)
        square(0, E - 1)
        for e in range(0, E, 2):
            acc = psum.tile([P, 2, C], F32, name="pair")
            for d in range(2):
                multiply(1, e + d, acc[:, d, :])
        for e in range(E):
            rectify(1, e)
            if e > 0:
                square(1, e - 1)
        square(1, E - 1)
        for h in range(HALVES):
            for t0, t1 in CHUNKS[h]:
                if h == HALVES - 1 and t1 == T:
                    combine_last(h, t0, t1)
                else:
                    combine(h, t0, t1)
